import numpy as np
import ml_dtypes


def mxq(x, axis, fmt="e4m3"):
    dtype, down = {"e4m3": (ml_dtypes.float8_e4m3fn, 7), "e5m2": (ml_dtypes.float8_e5m2, 14)}[fmt]
    v = np.moveaxis(np.asarray(x, np.float32).astype(ml_dtypes.bfloat16).astype(np.float64), axis, -1)
    blocks = v.reshape(v.shape[:-1] + (-1, 32))
    amax = np.abs(blocks).max(-1, keepdims=True)
    byte = np.maximum(np.where(amax > 0, np.frexp(amax)[1] - 1 + 127, 0) - down, 1)
    scale = np.exp2(byte - 127.0)
    codes = (blocks / scale).astype(np.float32).astype(dtype).astype(np.float64)
    return np.moveaxis((codes * scale).reshape(v.shape), -1, axis)


WIDE = False


def mx_kscale(k):
    if not WIDE:
        return np.ones(k)
    levels = np.array([10, -10, 5, -5, 0])
    if k % 512:
        return np.exp2(np.random.permutation(np.resize(levels, k // 32))).repeat(32)
    a = np.empty((k // 512, 16))
    for p in range(k // 512):
        a[p, :8] = np.random.permutation(np.resize(levels, 8))
        for g in range(8):
            far = levels[np.abs(levels - a[p, g]) >= 10]
            a[p, g + 8] = far[np.random.randint(len(far))]
    return np.exp2(a.ravel()).repeat(32)


def f64(x):
    return np.asarray(x).astype(np.float64)


def striped(idx):
    return np.tile(idx.reshape(-1, 16).T, (8, 1)).astype(np.uint16)


def unstriped(offs):
    return offs[:16].T.reshape(-1).astype(np.int64)


def striped8(idx):
    return np.concatenate([x.reshape(-1, 16).T for x in idx]).astype(np.uint16)


def runs(offs, k):
    lists = np.stack([offs[16 * r : 16 * r + 16].T.reshape(-1) for r in range(8)]).astype(np.int64)
    return lists[np.arange(k) % 512 // 64]


def pack_weight(w):
    k, n = w.shape
    w = f64(np.asarray(w, np.float32).astype(ml_dtypes.bfloat16)).reshape(k // 32, 32, n)
    amax = np.abs(w).max(1)
    byte = np.clip(np.where(amax > 0, np.frexp(amax)[1] - 1 + 127 - 7, 1), 1, 254)
    scaled = (w * np.exp2(127.0 - byte)[:, None, :]).reshape(k, n).astype(np.float32)
    words = np.ascontiguousarray(scaled.reshape(k // 512, 128, 4, n).transpose(0, 1, 3, 2)).astype(ml_dtypes.float8_e4m3fn).view(np.uint8)
    return words, np.ascontiguousarray(byte.astype(np.uint8).reshape(k // 512, 16, n))


def unpack_weight(words, scales):
    g, p, n, _ = words.shape
    vals = np.ascontiguousarray(words).view(ml_dtypes.float8_e4m3fn).astype(np.float64) * np.repeat(np.exp2(scales.astype(np.float64) - 127.0), 8, axis=1)[..., None]
    return vals.transpose(0, 1, 3, 2).reshape(g * 512, n)


def sigmoid(v):
    return 1.0 / (1.0 + np.exp(-np.maximum(v, -700.0)))


K, T, S, N, H, W = 512, 2048, 512, 512, 512, 1024


def setup_inputs():
    n = np.random.standard_normal
    s = mx_kscale(K)[:, None]
    u = mx_kscale(S)
    packed_xT = pack_weight(n((K, T)) * s)
    return {
        "x_words": packed_xT[0],
        "x_scales": packed_xT[1],
        "wa": (n((K, H)) / np.sqrt(K) / s).astype(np.float32),
        "gt": (np.random.uniform(0.5, 1.5, (S, 1)) * u[:, None]).astype(np.float32),
        "w1": (n((S, H)) / np.sqrt(S) / u[:, None]).astype(np.float32),
        "gp": (np.random.uniform(0.5, 1.5, (H, 1)) * u[:, None]).astype(np.float32),
        "res": (1.5 * n((N, H))).astype(np.float32),
        "w2": (n((H, N)) / np.sqrt(H) / u[:, None]).astype(np.float32),
        "offs": striped(np.random.permutation(T)[:S]),
        "n1": striped(np.random.randint(0, H, W)),
        "n2": striped8(np.stack([np.random.permutation(H) for _ in range(8)])),
        "n3": striped8(np.stack([np.random.permutation(H) for _ in range(8)])),
    }


def reference(x_words, x_scales, wa, gt, w1, gp, res, w2, offs, n1, n2, n3):
    xq = unpack_weight(x_words, x_scales)[:, unstriped(offs)]
    y = xq.T @ mxq(f64(wa), 0, "e4m3")
    mb = y[:, unstriped(n1)]
    mn = mb.reshape(S, H, 2).min(axis=2)
    mx = mb.reshape(S, H, 2).max(axis=2)
    z = f64(gt) * ((y - mn) * sigmoid(mx))
    h = mxq(f64(w1), 0, "e4m3").T @ mxq(z, 0, "e4m3")
    z2 = f64(gp) * (h[np.arange(H)[:, None], runs(n2, H)] + 0.75 * (h[np.arange(H)[:, None], runs(n3, H)]))
    return f64(res) + (mxq(f64(w2), 0, "e4m3").T @ mxq(z2, 0, "e4m3"))

@@ -1,0 +1,277 @@
+from contextlib import ExitStack
+
+import concourse.mybir as mybir
+
+K, T, S, N, H, W = 512, 2048, 512, 512, 512, 1024
+FLOPS = 2 * K * S * H + 2 * S * H * H + 2 * H * N * H
+
+F32 = mybir.dt.float32
+BF16 = mybir.dt.bfloat16
+I32 = mybir.dt.int32
+U32 = mybir.dt.uint32
+U16 = mybir.dt.uint16
+U8 = mybir.dt.uint8
+FP8X4 = mybir.dt.float8_e4m3fn_x4
+ALU = mybir.AluOpType
+ACT = mybir.ActivationFunctionType
+
+P = 128
+PACK = 4
+CH = 128
+NCH = H // CH
+HALF = H // 2
+
+
+def tile_picked_tok2ghardsum_none_p_kernel(
+    tc, x_words, x_scales, wa, gt, w1, gp, res, w2, offs, n1, n2, n3, out
+):
+    nc = tc.nc
+    with ExitStack() as ctx:
+        keep = ctx.enter_context(tc.tile_pool(name="keep", bufs=1))
+        ring = ctx.enter_context(tc.tile_pool(name="ring", bufs=2))
+        psum = ctx.enter_context(tc.psum_pool(name="psum", bufs=4))
+
+        def held(shape, dtype, name):
+            return keep.tile(shape, dtype, name=name, align_bytes=64)
+
+        def weave(engine_copy, dst, src):
+            engine_copy(
+                dst.rearrange("p (c i) t -> p c t i", i=4),
+                src.rearrange("p t (c i) -> p c t i", i=4),
+            )
+
+        def quantize(codes, scales, woven):
+            nc.vector.quantize_mx(out=codes.bitcast(FP8X4), scales=scales, in_=woven.rearrange("p c t -> p (c t)"))
+
+        offs_t = held([P, S // 16], U16, "offs_t")
+        n1_t = held([P, W // 16], U16, "n1_t")
+        n2_t = held([P, H // 16], U16, "n2_t")
+        n3_t = held([P, H // 16], U16, "n3_t")
+        xw_all = held([P, T], U32, "xw_all")
+        xs_all = held([P, T], U8, "xs_all")
+        wa_raw = [held([P, PACK, HALF], F32, f"wa_raw{a}") for a in range(2)]
+        w1_raw = held([P, PACK, H], F32, "w1_raw")
+        w2_raw = held([P, PACK, N], F32, "w2_raw")
+        res_t = held([P, PACK, H], F32, "res_t")
+        gt_t = held([P, PACK], F32, "gt_t")
+        gp_t = held([P, PACK], F32, "gp_t")
+
+        nc.vector.memset(xs_all[:].bitcast(I32), 0)
+        nc.sync.dma_start(offs_t[:], offs)
+        nc.sync.dma_start(xw_all[:].bitcast(I32), x_words[0].rearrange("p n t -> p (n t)").bitcast(I32))
+        for q in range(4):
+            nc.scalar.dma_start(
+                xs_all[32 * q : 32 * q + 4, :].bitcast(I32), x_scales[0, 4 * q : 4 * q + 4, :].bitcast(I32)
+            )
+        wa_rows = wa.rearrange("(p t) c -> p t c", t=PACK)
+        for a in range(2):
+            nc.sync.dma_start(wa_raw[a][:], wa_rows[:, :, a * HALF : (a + 1) * HALF])
+        nc.sync.dma_start(n1_t[:], n1)
+        nc.sync.dma_start(w1_raw[:], w1.rearrange("(p t) c -> p t c", t=PACK))
+        nc.sync.dma_start(gt_t[:], gt.rearrange("(p t) o -> p (t o)", t=PACK))
+        nc.sync.dma_start(gp_t[:], gp.rearrange("(p t) o -> p (t o)", t=PACK))
+        nc.sync.dma_start(n3_t[:], n3)
+        nc.sync.dma_start(n2_t[:], n2)
+        nc.sync.dma_start(w2_raw[:], w2.rearrange("(p t) c -> p t c", t=PACK))
+        nc.sync.dma_start(res_t[:], res.rearrange("(u p) c -> p u c", p=P))
+
+        xs = held([P, S], U8, "xs")
+        xw = held([P, S], U32, "xw")
+        nc.vector.tensor_copy(xs[:].rearrange("p (t m) -> p m t", t=PACK), xs_all[:].indirect(offs_t[:]))
+        nc.vector.tensor_copy(xw[:].rearrange("p (t m) -> p m t", t=PACK), xw_all[:].indirect(offs_t[:]))
+
+        y_bank = [psum.tile([P, H], F32, name=f"y_bank{t}", tag="wide") for t in range(PACK)]
+        y = [held([P, H], F32, f"y{t}") for t in range(PACK)]
+        SPLIT = 96
+        for a in range(2):
+            woven = held([P, HALF, PACK], BF16, f"wa_woven{a}")
+            codes = held([P, HALF], U32, f"wa_codes{a}")
+            scales = held([P, HALF], U8, f"wa_scales{a}")
+            if a == 0:
+                nc.scalar.activation(
+                    woven[:].rearrange("p (c i) t -> p c t i", i=4),
+                    wa_raw[a][:].rearrange("p t (c i) -> p c t i", i=4),
+                    ACT.Copy,
+                )
+            else:
+                weave(nc.scalar.copy, woven[:, :SPLIT, :], wa_raw[a][:, :, :SPLIT])
+                weave(nc.vector.tensor_copy, woven[:, SPLIT:, :], wa_raw[a][:, :, SPLIT:])
+            quantize(codes[:], scales[:], woven[:])
+            for t in range(PACK):
+                nc.tensor.matmul_mx(
+                    out=y_bank[t][:, a * HALF : (a + 1) * HALF],
+                    lhsT=xw[:, t * P : (t + 1) * P].bitcast(FP8X4),
+                    lhsT_scale=xs[:, t * P : (t + 1) * P],
+                    rhs=codes[:].bitcast(FP8X4),
+                    rhs_scale=scales[:],
+                    start=True,
+                    stop=True,
+                )
+            nc.scalar.copy(y[0][:, a * HALF : (a + 1) * HALF], y_bank[0][:, a * HALF : (a + 1) * HALF])
+        for t in range(1, PACK):
+            nc.vector.tensor_copy(y[t][:], y_bank[t][:])
+
+        w1_woven = held([P, H, PACK], BF16, "w1_woven")
+        w1_codes = held([P, H], U32, "w1_codes")
+        w1_scales = held([P, H], U8, "w1_scales")
+        w2_codes = held([P, N], U32, "w2_codes")
+        w2_scales = held([P, N], U8, "w2_scales")
+        h = [held([P, H], F32, f"h{t}") for t in range(PACK)]
+
+        members, larger, smaller, gate, diff, z_flat, z_woven, h_bank = {}, {}, {}, {}, {}, {}, {}, {}
+
+        def fetch_members(c):
+            members[c] = ring.tile([P, PACK, 2 * CH], F32, name="members", align_bytes=64)
+            for t in range(PACK):
+                nc.scalar.activation(
+                    members[c][:, t, :], y[t][:].indirect(n1_t[:, c * 16 : (c + 1) * 16]), ACT.Copy
+                )
+
+        def extremes(c):
+            pairs = members[c][:].rearrange("p t (j e) -> p (t j) e", e=2)
+            larger[c] = ring.tile([P, PACK * CH], F32, name="larger", align_bytes=64)
+            smaller[c] = ring.tile([P, PACK, CH], F32, name="smaller", align_bytes=64)
+            nc.vector.tensor_tensor(larger[c][:], pairs[:, :, 0], pairs[:, :, 1], ALU.max)
+            nc.vector.tensor_tensor(
+                smaller[c][:].rearrange("p t j -> p (t j)"), pairs[:, :, 0], pairs[:, :, 1], ALU.min
+            )
+
+        def sigmoid(c):
+            gate[c] = ring.tile([P, PACK, CH], F32, name="gate", align_bytes=64)
+            nc.scalar.activation(gate[c][:].rearrange("p t j -> p (t j)"), larger[c][:], ACT.Sigmoid)
+
+        def differences(c):
+            diff[c] = ring.tile([P, PACK, CH], F32, name="diff", align_bytes=64)
+            for t in range(PACK):
+                nc.vector.tensor_tensor(
+                    diff[c][:, t, :], y[t][:, c * CH : (c + 1) * CH], smaller[c][:, t, :], ALU.subtract
+                )
+
+        def make_z(c):
+            z_flat[c] = ring.tile([P, PACK, CH], BF16, name="z_flat", align_bytes=64)
+            for t in range(PACK):
+                nc.vector.scalar_tensor_tensor(
+                    z_flat[c][:, t, :], diff[c][:, t, :], gt_t[:, t : t + 1], gate[c][:, t, :], ALU.mult, ALU.mult
+                )
+
+        def weave_z(c):
+            if c + 1 < NCH:
+                z_woven[c] = ring.tile([P, CH, PACK], BF16, name="z_woven", align_bytes=64)
+            else:
+                z_woven[c] = keep.tile([P, CH, PACK], BF16, name="z_woven_last", tag="late", align_bytes=64)
+            weave(nc.vector.tensor_copy, z_woven[c][:], z_flat[c][:])
+
+        def second_product(c):
+            codes = held([P, CH], U32, f"z_codes{c}")
+            scales = held([P, CH], U8, f"z_scales{c}")
+            quantize(codes[:], scales[:], z_woven[c][:])
+            h_bank[c] = psum.tile([P, PACK, CH], F32, name="h_bank", tag="h_bank")
+            for t in range(PACK):
+                nc.tensor.matmul_mx(
+                    out=h_bank[c][:, t, :],
+                    lhsT=w1_codes[:, t * P : (t + 1) * P].bitcast(FP8X4),
+                    lhsT_scale=w1_scales[:, t * P : (t + 1) * P],
+                    rhs=codes[:].bitcast(FP8X4),
+                    rhs_scale=scales[:],
+                    start=True,
+                    stop=True,
+                )
+
+        def drain_h(c):
+            for t in range(PACK):
+                nc.scalar.activation(
+                    h[t][:, c * CH : (c + 1) * CH], h_bank[c][:, t, :], ACT.Copy, scale=gp_t[:, t : t + 1]
+                )
+
+        fetch_members(0)
+        nc.vector.tensor_copy(
+            w1_woven[:].rearrange("p (t m) j -> p m j t", t=PACK),
+            w1_raw[:].rearrange("p j (m t) -> p m j t", t=PACK),
+        )
+        fetch_members(1)
+        extremes(0)
+        quantize(w1_codes[:], w1_scales[:], w1_woven[:])
+        sigmoid(0)
+        differences(0)
+        for c in range(1, NCH):
+            if c + 1 < NCH:
+                fetch_members(c + 1)
+            extremes(c)
+            make_z(c - 1)
+            sigmoid(c)
+            weave_z(c - 1)
+            differences(c)
+            second_product(c - 1)
+        make_z(NCH - 1)
+        for c in range(NCH - 1):
+            drain_h(c)
+        weave_z(NCH - 1)
+        second_product(NCH - 1)
+        drain_h(NCH - 1)
+
+        out_rows = out.rearrange("(u p) c -> p u c", p=P)
+        third, second, z2_woven, o_bank = {}, {}, {}, {}
+
+        def fetch_n3(c):
+            third[c] = held([P, PACK, CH], F32, f"third{c}")
+            for t in range(PACK):
+                nc.scalar.activation(
+                    third[c][:, t, :], h[t][:].indirect(n3_t[:, c * 8 : (c + 1) * 8]), ACT.Copy, scale=0.75
+                )
+
+        def fetch_n2(c):
+            second[c] = held([P, PACK, CH], F32, f"second{c}")
+            for t in range(PACK):
+                window = h[t][:].indirect(n2_t[:, c * 8 : (c + 1) * 8])
+                if c < ON_VECTOR:
+                    nc.vector.tensor_copy(second[c][:, t, :], window)
+                else:
+                    nc.scalar.activation(second[c][:, t, :], window, ACT.Copy)
+
+        def weave_z2(c):
+            z2_woven[c] = ring.tile([P, CH, PACK], BF16, name="z2_woven", align_bytes=64)
+            nc.vector.tensor_tensor(
+                z2_woven[c][:].rearrange("p (c i) t -> p c t i", i=2),
+                second[c][:].rearrange("p t (c i) -> p c t i", i=2),
+                third[c][:].rearrange("p t (c i) -> p c t i", i=2),
+                ALU.add,
+            )
+
+        def third_product(c):
+            codes = held([P, CH], U32, f"z2_codes{c}")
+            scales = held([P, CH], U8, f"z2_scales{c}")
+            quantize(codes[:], scales[:], z2_woven[c][:])
+            o_bank[c] = psum.tile([P, PACK, CH], F32, name=f"o_bank{c}", tag="wide")
+            for u in range(PACK):
+                nc.tensor.matmul_mx(
+                    out=o_bank[c][:, u, :],
+                    lhsT=w2_codes[:, u * P : (u + 1) * P].bitcast(FP8X4),
+                    lhsT_scale=w2_scales[:, u * P : (u + 1) * P],
+                    rhs=codes[:].bitcast(FP8X4),
+                    rhs_scale=scales[:],
+                    start=True,
+                    stop=True,
+                )
+
+        def finish(c):
+            result = held([P, PACK, CH], F32, f"result{c}")
+            nc.vector.tensor_tensor(result[:], o_bank[c][:], res_t[:, :, c * CH : (c + 1) * CH], ALU.add)
+            nc.sync.dma_start(out_rows[:, :, c * CH : (c + 1) * CH], result[:])
+
+        ON_VECTOR = 2
+        fetch_n3(0)
+        fetch_n2(0)
+        w2_woven = keep.tile([P, N, PACK], BF16, name="w2_woven", tag="late", align_bytes=64)
+        weave(nc.vector.tensor_copy, w2_woven[:], w2_raw[:])
+        weave_z2(0)
+        quantize(w2_codes[:], w2_scales[:], w2_woven[:])
+        for c in range(1, NCH):
+            fetch_n3(c)
+            third_product(c - 1)
+            fetch_n2(c)
+            weave_z2(c)
+            if c >= 2:
+                finish(c - 2)
+        third_product(NCH - 1)
+        finish(NCH - 2)
+        finish(NCH - 1)

@@ -17,9 +17,12 @@ ACT = mybir.ActivationFunctionType
 
 P = 128
 PACK = 4
-CH = 128
-NCH = H // CH
 HALF = H // 2
+SPLIT = 192
+B_CHUNKS = [128,128,128,128]
+C_CHUNKS = [128,128,128,128]
+ON_VECTOR = 10
+LAG = 3
 
 
 def tile_picked_tok2ghardsum_none_p_kernel(
@@ -28,11 +31,12 @@ def tile_picked_tok2ghardsum_none_p_kernel(
     nc = tc.nc
     with ExitStack() as ctx:
         keep = ctx.enter_context(tc.tile_pool(name="keep", bufs=1))
-        ring = ctx.enter_context(tc.tile_pool(name="ring", bufs=2))
+        ring = ctx.enter_context(tc.tile_pool(name="ring", bufs=4))
+        shared = ctx.enter_context(tc.tile_pool(name="shared", bufs=1))
         psum = ctx.enter_context(tc.psum_pool(name="psum", bufs=4))
 
-        def held(shape, dtype, name):
-            return keep.tile(shape, dtype, name=name, align_bytes=64)
+        def held(shape, dtype, name, tag=None):
+            return keep.tile(shape, dtype, name=name, tag=tag or name, align_bytes=64)
 
         def weave(engine_copy, dst, src):
             engine_copy(
@@ -42,6 +46,17 @@ def tile_picked_tok2ghardsum_none_p_kernel(
 
         def quantize(codes, scales, woven):
             nc.vector.quantize_mx(out=codes.bitcast(FP8X4), scales=scales, in_=woven.rearrange("p c t -> p (c t)"))
+
+        def product(acc, left_codes, left_scales, t, codes, scales):
+            nc.tensor.matmul_mx(
+                out=acc,
+                lhsT=left_codes[:, t * P : (t + 1) * P].bitcast(FP8X4),
+                lhsT_scale=left_scales[:, t * P : (t + 1) * P],
+                rhs=codes[:].bitcast(FP8X4),
+                rhs_scale=scales[:],
+                start=True,
+                stop=True,
+            )
 
         offs_t = held([P, S // 16], U16, "offs_t")
         n1_t = held([P, W // 16], U16, "n1_t")
@@ -55,17 +70,17 @@ def tile_picked_tok2ghardsum_none_p_kernel(
         res_t = held([P, PACK, H], F32, "res_t")
         gt_t = held([P, PACK], F32, "gt_t")
         gp_t = held([P, PACK], F32, "gp_t")
+        nc.gpsimd.memset(xs_all[:].bitcast(I32), 0)
 
-        nc.vector.memset(xs_all[:].bitcast(I32), 0)
+        wa_rows = wa.rearrange("(p t) c -> p t c", t=PACK)
         nc.sync.dma_start(offs_t[:], offs)
+        nc.sync.dma_start(wa_raw[0][:], wa_rows[:, :, :HALF])
         nc.sync.dma_start(xw_all[:].bitcast(I32), x_words[0].rearrange("p n t -> p (n t)").bitcast(I32))
         for q in range(4):
             nc.scalar.dma_start(
-                xs_all[32 * q : 32 * q + 4, :].bitcast(I32), x_scales[0, 4 * q : 4 * q + 4, :].bitcast(I32)
+                xs_all[q : P : 32, :].bitcast(I32), x_scales[0, q : 16 : 4, :].bitcast(I32)
             )
-        wa_rows = wa.rearrange("(p t) c -> p t c", t=PACK)
-        for a in range(2):
-            nc.sync.dma_start(wa_raw[a][:], wa_rows[:, :, a * HALF : (a + 1) * HALF])
+        nc.sync.dma_start(wa_raw[1][:], wa_rows[:, :, HALF:])
         nc.sync.dma_start(n1_t[:], n1)
         nc.sync.dma_start(w1_raw[:], w1.rearrange("(p t) c -> p t c", t=PACK))
         nc.sync.dma_start(gt_t[:], gt.rearrange("(p t) o -> p (t o)", t=PACK))
@@ -75,18 +90,20 @@ def tile_picked_tok2ghardsum_none_p_kernel(
         nc.sync.dma_start(w2_raw[:], w2.rearrange("(p t) c -> p t c", t=PACK))
         nc.sync.dma_start(res_t[:], res.rearrange("(u p) c -> p u c", p=P))
 
-        xs = held([P, S], U8, "xs")
-        xw = held([P, S], U32, "xw")
-        nc.vector.tensor_copy(xs[:].rearrange("p (t m) -> p m t", t=PACK), xs_all[:].indirect(offs_t[:]))
-        nc.vector.tensor_copy(xw[:].rearrange("p (t m) -> p m t", t=PACK), xw_all[:].indirect(offs_t[:]))
+        warm = held([P, 2], F32, "warm")
+        nc.gpsimd.memset(warm[:, 0:1], 0.0)
+        nc.scalar.activation(warm[:, 1:2], warm[:, 0:1], ACT.Sigmoid)
 
-        y_bank = [psum.tile([P, H], F32, name=f"y_bank{t}", tag="wide") for t in range(PACK)]
-        y = [held([P, H], F32, f"y{t}") for t in range(PACK)]
-        SPLIT = 96
+        xs = held([P, S], U8, "xs")
+        nc.vector.tensor_copy(xs[:].rearrange("p (t m) -> p m t", t=PACK), xs_all[:].indirect(offs_t[:]))
+
+        y = [held([P, H], F32, f"y{t}", tag="wa_raw1" if t == 0 else None) for t in range(PACK)]
+        wa_codes = held([P, H], U32, "wa_codes")
+        wa_scales = held([P, H], U8, "wa_scales")
         for a in range(2):
             woven = held([P, HALF, PACK], BF16, f"wa_woven{a}")
-            codes = held([P, HALF], U32, f"wa_codes{a}")
-            scales = held([P, HALF], U8, f"wa_scales{a}")
+            codes = wa_codes[:, a * HALF : (a + 1) * HALF]
+            scales = wa_scales[:, a * HALF : (a + 1) * HALF]
             if a == 0:
                 nc.scalar.activation(
                     woven[:].rearrange("p (c i) t -> p c t i", i=4),
@@ -96,140 +113,150 @@ def tile_picked_tok2ghardsum_none_p_kernel(
             else:
                 weave(nc.scalar.copy, woven[:, :SPLIT, :], wa_raw[a][:, :, :SPLIT])
                 weave(nc.vector.tensor_copy, woven[:, SPLIT:, :], wa_raw[a][:, :, SPLIT:])
-            quantize(codes[:], scales[:], woven[:])
-            for t in range(PACK):
-                nc.tensor.matmul_mx(
-                    out=y_bank[t][:, a * HALF : (a + 1) * HALF],
-                    lhsT=xw[:, t * P : (t + 1) * P].bitcast(FP8X4),
-                    lhsT_scale=xs[:, t * P : (t + 1) * P],
-                    rhs=codes[:].bitcast(FP8X4),
-                    rhs_scale=scales[:],
-                    start=True,
-                    stop=True,
-                )
-            nc.scalar.copy(y[0][:, a * HALF : (a + 1) * HALF], y_bank[0][:, a * HALF : (a + 1) * HALF])
-        for t in range(1, PACK):
-            nc.vector.tensor_copy(y[t][:], y_bank[t][:])
+            quantize(codes, scales, woven[:])
+            if a == 0:
+                xw = held([P, S], U32, "xw", tag="wa_woven0")
+                nc.vector.tensor_copy(xw[:].rearrange("p (t m) -> p m t", t=PACK), xw_all[:].indirect(offs_t[:]))
+        for t in range(PACK):
+            copy = nc.scalar.copy if t in [0,3] else nc.vector.tensor_copy
+            bank = psum.tile([P, H], F32, name="y_bank", tag="wide")
+            step = HALF if t < 2 else H
+            for first in range(0, H, step):
+                cols = slice(first, first + step)
+                if t == 0 and first == 0:
+                    early = psum.tile([P, HALF], F32, name="y_early", tag="h_bank")
+                    product(early[:], xw, xs, t, wa_codes[:, cols], wa_scales[:, cols])
+                    copy(y[t][:, cols], early[:])
+                else:
+                    product(bank[:, cols], xw, xs, t, wa_codes[:, cols], wa_scales[:, cols])
+            rest = slice(HALF if t == 0 else 0, H)
+            copy(y[t][:, rest], bank[:, rest])
 
-        w1_woven = held([P, H, PACK], BF16, "w1_woven")
+        w1_woven = held([P, H, PACK], BF16, "w1_woven", tag="wa_codes")
         w1_codes = held([P, H], U32, "w1_codes")
         w1_scales = held([P, H], U8, "w1_scales")
         w2_codes = held([P, N], U32, "w2_codes")
         w2_scales = held([P, N], U8, "w2_scales")
-        h = [held([P, H], F32, f"h{t}") for t in range(PACK)]
-
-        members, larger, smaller, gate, diff, z_flat, z_woven, h_bank = {}, {}, {}, {}, {}, {}, {}, {}
-
-        def fetch_members(c):
-            members[c] = ring.tile([P, PACK, 2 * CH], F32, name="members", align_bytes=64)
-            for t in range(PACK):
-                nc.scalar.activation(
-                    members[c][:, t, :], y[t][:].indirect(n1_t[:, c * 16 : (c + 1) * 16]), ACT.Copy
-                )
-
-        def extremes(c):
-            pairs = members[c][:].rearrange("p t (j e) -> p (t j) e", e=2)
-            larger[c] = ring.tile([P, PACK * CH], F32, name="larger", align_bytes=64)
-            smaller[c] = ring.tile([P, PACK, CH], F32, name="smaller", align_bytes=64)
-            nc.vector.tensor_tensor(larger[c][:], pairs[:, :, 0], pairs[:, :, 1], ALU.max)
-            nc.vector.tensor_tensor(
-                smaller[c][:].rearrange("p t j -> p (t j)"), pairs[:, :, 0], pairs[:, :, 1], ALU.min
-            )
-
-        def sigmoid(c):
-            gate[c] = ring.tile([P, PACK, CH], F32, name="gate", align_bytes=64)
-            nc.scalar.activation(gate[c][:].rearrange("p t j -> p (t j)"), larger[c][:], ACT.Sigmoid)
-
-        def differences(c):
-            diff[c] = ring.tile([P, PACK, CH], F32, name="diff", align_bytes=64)
-            for t in range(PACK):
-                nc.vector.tensor_tensor(
-                    diff[c][:, t, :], y[t][:, c * CH : (c + 1) * CH], smaller[c][:, t, :], ALU.subtract
-                )
-
-        def make_z(c):
-            z_flat[c] = ring.tile([P, PACK, CH], BF16, name="z_flat", align_bytes=64)
-            for t in range(PACK):
-                nc.vector.scalar_tensor_tensor(
-                    z_flat[c][:, t, :], diff[c][:, t, :], gt_t[:, t : t + 1], gate[c][:, t, :], ALU.mult, ALU.mult
-                )
-
-        def weave_z(c):
-            if c + 1 < NCH:
-                z_woven[c] = ring.tile([P, CH, PACK], BF16, name="z_woven", align_bytes=64)
-            else:
-                z_woven[c] = keep.tile([P, CH, PACK], BF16, name="z_woven_last", tag="late", align_bytes=64)
-            weave(nc.vector.tensor_copy, z_woven[c][:], z_flat[c][:])
-
-        def second_product(c):
-            codes = held([P, CH], U32, f"z_codes{c}")
-            scales = held([P, CH], U8, f"z_scales{c}")
-            quantize(codes[:], scales[:], z_woven[c][:])
-            h_bank[c] = psum.tile([P, PACK, CH], F32, name="h_bank", tag="h_bank")
-            for t in range(PACK):
-                nc.tensor.matmul_mx(
-                    out=h_bank[c][:, t, :],
-                    lhsT=w1_codes[:, t * P : (t + 1) * P].bitcast(FP8X4),
-                    lhsT_scale=w1_scales[:, t * P : (t + 1) * P],
-                    rhs=codes[:].bitcast(FP8X4),
-                    rhs_scale=scales[:],
-                    start=True,
-                    stop=True,
-                )
-
-        def drain_h(c):
-            for t in range(PACK):
-                nc.scalar.activation(
-                    h[t][:, c * CH : (c + 1) * CH], h_bank[c][:, t, :], ACT.Copy, scale=gp_t[:, t : t + 1]
-                )
-
-        fetch_members(0)
+        last_larger = shared.tile([P, PACK, H], F32, name="last_larger", offset=0)
+        h_banks = []
         nc.vector.tensor_copy(
             w1_woven[:].rearrange("p (t m) j -> p m j t", t=PACK),
             w1_raw[:].rearrange("p j (m t) -> p m j t", t=PACK),
         )
-        fetch_members(1)
-        extremes(0)
         quantize(w1_codes[:], w1_scales[:], w1_woven[:])
-        sigmoid(0)
-        differences(0)
-        for c in range(1, NCH):
-            if c + 1 < NCH:
-                fetch_members(c + 1)
-            extremes(c)
-            make_z(c - 1)
-            sigmoid(c)
-            weave_z(c - 1)
-            differences(c)
-            second_product(c - 1)
-        make_z(NCH - 1)
-        for c in range(NCH - 1):
-            drain_h(c)
-        weave_z(NCH - 1)
-        second_product(NCH - 1)
-        drain_h(NCH - 1)
+
+        b_start = [sum(B_CHUNKS[:c]) for c in range(len(B_CHUNKS))]
+        units = [(c, t) for c in range(len(B_CHUNKS)) for t in range(PACK)]
+        z_flat = [held([P, PACK, width], BF16, f"z_flat{c}") for c, width in enumerate(B_CHUNKS)]
+        gate, diff, smaller = {}, {}, {}
+
+        def extremes(c, t):
+            width = B_CHUNKS[c]
+            members = ring.tile([P, 2 * width], F32, name="members", align_bytes=64)
+            for e in range(0, 2 * width, 256):
+                n = min(256, 2 * width - e)
+                first = (2 * b_start[c] + e) // 16
+                nc.scalar.activation(
+                    members[:, e : e + n], y[t][:].indirect(n1_t[:, first : first + n // 16]), ACT.Copy
+                )
+            pairs = members[:].rearrange("p (j e) -> p j e", e=2)
+            if c + 1 < len(B_CHUNKS):
+                larger = held([P, width], F32, f"larger{c}_{t}")[:]
+            else:
+                larger = last_larger[:, t, :width]
+            smaller[c, t] = held([P, width], F32, f"smaller{c}_{t}")
+            gate[c, t] = held([P, width], F32, f"gate{c}_{t}")
+            nc.vector.tensor_tensor(larger, pairs[:, :, 0], pairs[:, :, 1], ALU.max)
+            nc.vector.tensor_tensor(smaller[c, t][:], pairs[:, :, 0], pairs[:, :, 1], ALU.min)
+            nc.scalar.activation(gate[c, t][:], larger, ACT.Sigmoid)
+
+        def difference(c, t):
+            width = B_CHUNKS[c]
+            diff[c, t] = held([P, width], F32, f"diff{c}_{t}")
+            nc.vector.tensor_tensor(
+                diff[c, t][:], y[t][:, b_start[c] : b_start[c] + width], smaller[c, t][:], ALU.subtract
+            )
+
+        def make_z(c, t):
+            nc.vector.scalar_tensor_tensor(
+                z_flat[c][:, t, :], diff[c, t][:], gt_t[:, t : t + 1], gate[c, t][:], ALU.mult, ALU.mult
+            )
+
+        def second_product(c):
+            width = B_CHUNKS[c]
+            last = c + 1 == len(B_CHUNKS)
+            woven = held([P, width, PACK], BF16, f"z_woven{c}", tag="late" if last else None)
+            weave(nc.vector.tensor_copy, woven[:], z_flat[c][:])
+            codes = held([P, width], U32, f"z_codes{c}")
+            scales = held([P, width], U8, f"z_scales{c}")
+            return woven, codes, scales
+
+        def second_matmuls(c, woven, codes, scales):
+            width = B_CHUNKS[c]
+            quantize(codes[:], scales[:], woven[:])
+            last = c + 1 == len(B_CHUNKS)
+            per_bank = 1 if last else H // width
+            for t0 in range(0, PACK, per_bank):
+                ts = range(t0, min(PACK, t0 + per_bank))
+                bank = psum.tile([P, len(ts), width], F32, name="h_bank", tag="wide" if last else "h_bank")
+                for t in ts:
+                    product(bank[:, t - t0, :], w1_codes, w1_scales, t, codes, scales)
+                h_banks.extend((c, t, bank[:, t - t0, :]) for t in ts)
+
+        staged = {}
+        for u in range(len(units) + LAG + 2):
+            if u < len(units):
+                extremes(*units[u])
+            if 0 <= u - LAG - 2 < len(units) and units[u - LAG - 2][1] == PACK - 1:
+                c = units[u - LAG - 2][0]
+                second_matmuls(c, *staged[c])
+            if 0 <= u - LAG - 1 < len(units) and units[u - LAG - 1][1] == PACK - 1:
+                c = units[u - LAG - 1][0]
+                staged[c] = second_product(c)
+            if 0 <= u - LAG < len(units):
+                make_z(*units[u - LAG])
+            if 0 <= u - 1 < len(units):
+                difference(*units[u - 1])
+
+        for a, (copy, tag) in enumerate(((nc.scalar.copy, "gate3_0"), (nc.vector.tensor_copy, "late"))):
+            cols = slice(a * HALF, (a + 1) * HALF)
+            w2_woven = held([P, HALF, PACK], BF16, f"w2_woven{a}", tag=tag)
+            weave(copy, w2_woven[:], w2_raw[:, :, cols])
+            quantize(w2_codes[:, cols], w2_scales[:, cols], w2_woven[:])
+        h = [shared.tile([P, H], F32, name=f"h{t}", offset=t * H * 4) for t in range(PACK)]
+        for c, t, sums in h_banks:
+            place = h[t][:, b_start[c] : b_start[c] + B_CHUNKS[c]]
+            if False:
+                nc.vector.tensor_scalar(place, sums, gp_t[:, t : t + 1], None, ALU.mult)
+            else:
+                nc.scalar.activation(place, sums, ACT.Copy, scale=gp_t[:, t : t + 1])
 
         out_rows = out.rearrange("(u p) c -> p u c", p=P)
+        c_start = [sum(C_CHUNKS[:c]) for c in range(len(C_CHUNKS))]
         third, second, z2_woven, o_bank = {}, {}, {}, {}
 
         def fetch_n3(c):
-            third[c] = held([P, PACK, CH], F32, f"third{c}")
+            width = C_CHUNKS[c]
+            first = c_start[c] // 16
+            third[c] = held([P, PACK, width], F32, f"third{c}")
             for t in range(PACK):
                 nc.scalar.activation(
-                    third[c][:, t, :], h[t][:].indirect(n3_t[:, c * 8 : (c + 1) * 8]), ACT.Copy, scale=0.75
+                    third[c][:, t, :], h[t][:].indirect(n3_t[:, first : first + width // 16]), ACT.Copy, scale=0.75
                 )
 
         def fetch_n2(c):
-            second[c] = held([P, PACK, CH], F32, f"second{c}")
+            width = C_CHUNKS[c]
+            first = c_start[c] // 16
+            second[c] = ring.tile([P, PACK, width], F32, name="second", align_bytes=64, bufs=2)
             for t in range(PACK):
-                window = h[t][:].indirect(n2_t[:, c * 8 : (c + 1) * 8])
-                if c < ON_VECTOR:
+                window = h[t][:].indirect(n2_t[:, first : first + width // 16])
+                if c + 1 < len(C_CHUNKS):
                     nc.vector.tensor_copy(second[c][:, t, :], window)
                 else:
                     nc.scalar.activation(second[c][:, t, :], window, ACT.Copy)
 
         def weave_z2(c):
-            z2_woven[c] = ring.tile([P, CH, PACK], BF16, name="z2_woven", align_bytes=64)
+            z2_woven[c] = held([P, C_CHUNKS[c], PACK], BF16, f"z2_woven{c}")
             nc.vector.tensor_tensor(
                 z2_woven[c][:].rearrange("p (c i) t -> p c t i", i=2),
                 second[c][:].rearrange("p t (c i) -> p c t i", i=2),
@@ -238,40 +265,34 @@ def tile_picked_tok2ghardsum_none_p_kernel(
             )
 
         def third_product(c):
-            codes = held([P, CH], U32, f"z2_codes{c}")
-            scales = held([P, CH], U8, f"z2_scales{c}")
+            width = C_CHUNKS[c]
+            codes = held([P, width], U32, f"z2_codes{c}")
+            scales = held([P, width], U8, f"z2_scales{c}")
             quantize(codes[:], scales[:], z2_woven[c][:])
-            o_bank[c] = psum.tile([P, PACK, CH], F32, name=f"o_bank{c}", tag="wide")
-            for u in range(PACK):
-                nc.tensor.matmul_mx(
-                    out=o_bank[c][:, u, :],
-                    lhsT=w2_codes[:, u * P : (u + 1) * P].bitcast(FP8X4),
-                    lhsT_scale=w2_scales[:, u * P : (u + 1) * P],
-                    rhs=codes[:].bitcast(FP8X4),
-                    rhs_scale=scales[:],
-                    start=True,
-                    stop=True,
-                )
+            per_bank = H // width if c + 2 < len(C_CHUNKS) else 2
+            o_bank[c] = []
+            for u0 in range(0, PACK, per_bank):
+                us = range(u0, min(PACK, u0 + per_bank))
+                bank = psum.tile([P, len(us), width], F32, name="o_bank", tag="wide")
+                o_bank[c].append((us, bank))
+                for u in us:
+                    product(bank[:, u - u0, :], w2_codes, w2_scales, u, codes, scales)
 
         def finish(c):
-            result = held([P, PACK, CH], F32, f"result{c}")
-            nc.vector.tensor_tensor(result[:], o_bank[c][:], res_t[:, :, c * CH : (c + 1) * CH], ALU.add)
-            nc.sync.dma_start(out_rows[:, :, c * CH : (c + 1) * CH], result[:])
+            cols = slice(c_start[c], c_start[c] + C_CHUNKS[c])
+            for us, bank in o_bank[c]:
+                result = held([P, len(us), C_CHUNKS[c]], F32, f"result{c}_{us.start}")
+                nc.vector.tensor_tensor(result[:], bank[:], res_t[:, us.start : us.stop, cols], ALU.add)
+                nc.sync.dma_start(out_rows[:, us.start : us.stop, cols], result[:])
 
-        ON_VECTOR = 2
-        fetch_n3(0)
-        fetch_n2(0)
-        w2_woven = keep.tile([P, N, PACK], BF16, name="w2_woven", tag="late", align_bytes=64)
-        weave(nc.vector.tensor_copy, w2_woven[:], w2_raw[:])
-        weave_z2(0)
-        quantize(w2_codes[:], w2_scales[:], w2_woven[:])
-        for c in range(1, NCH):
-            fetch_n3(c)
-            third_product(c - 1)
-            fetch_n2(c)
-            weave_z2(c)
+        last = len(C_CHUNKS) - 1
+        for c in range(len(C_CHUNKS) + 2):
+            if c <= last:
+                fetch_n3(c)
+                fetch_n2(c)
+            if 1 <= c <= last + 1:
+                third_product(c - 1)
+            if c <= last:
+                weave_z2(c)
             if c >= 2:
                 finish(c - 2)
-        third_product(NCH - 1)
-        finish(NCH - 2)
-        finish(NCH - 1)

@@ -18,7 +18,7 @@ ACT = mybir.ActivationFunctionType
 P = 128
 PACK = 4
 HALF = H // 2
-SPLIT = 192
+SPLIT = 112
 B_CHUNKS = [128,128,128,128]
 C_CHUNKS = [128,128,128,128]
 ON_VECTOR = 10
@@ -75,11 +75,11 @@ def tile_picked_tok2ghardsum_none_p_kernel(
         wa_rows = wa.rearrange("(p t) c -> p t c", t=PACK)
         nc.sync.dma_start(offs_t[:], offs)
         nc.sync.dma_start(wa_raw[0][:], wa_rows[:, :, :HALF])
-        nc.sync.dma_start(xw_all[:].bitcast(I32), x_words[0].rearrange("p n t -> p (n t)").bitcast(I32))
         for q in range(4):
-            nc.scalar.dma_start(
+            nc.sync.dma_start(
                 xs_all[q : P : 32, :].bitcast(I32), x_scales[0, q : 16 : 4, :].bitcast(I32)
             )
+        nc.sync.dma_start(xw_all[:].bitcast(I32), x_words[0].rearrange("p n t -> p (n t)").bitcast(I32))
         nc.sync.dma_start(wa_raw[1][:], wa_rows[:, :, HALF:])
         nc.sync.dma_start(n1_t[:], n1)
         nc.sync.dma_start(w1_raw[:], w1.rearrange("(p t) c -> p t c", t=PACK))
@@ -99,7 +99,7 @@ def tile_picked_tok2ghardsum_none_p_kernel(
 
         y = [held([P, H], F32, f"y{t}", tag="wa_raw1" if t == 0 else None) for t in range(PACK)]
         wa_codes = held([P, H], U32, "wa_codes")
-        wa_scales = held([P, H], U8, "wa_scales")
+        wa_scales = held([P, H], U8, "wa_scales", tag="xs_all")
         for a in range(2):
             woven = held([P, HALF, PACK], BF16, f"wa_woven{a}")
             codes = wa_codes[:, a * HALF : (a + 1) * HALF]

@@ -16,13 +16,17 @@ ALU = mybir.AluOpType
 ACT = mybir.ActivationFunctionType
 
 P = 128
-PACK = 4
+SLOTS = 4
+QUADRANT = 32
+PER_COLUMN = 16
 HALF = H // 2
-SPLIT = 112
-B_CHUNKS = [128,128,128,128]
-C_CHUNKS = [128,128,128,128]
-ON_VECTOR = 10
+CHUNK = 128
+CHUNKS = H // CHUNK
+LAST = CHUNKS - 1
+WA_ON_SCALAR = 112
+MEMBER_BUFS = 4
 LAG = 3
+SECOND_BUFS = 2
 
 
 def tile_picked_tok2ghardsum_none_p_kernel(
@@ -31,268 +35,248 @@ def tile_picked_tok2ghardsum_none_p_kernel(
     nc = tc.nc
     with ExitStack() as ctx:
         keep = ctx.enter_context(tc.tile_pool(name="keep", bufs=1))
-        ring = ctx.enter_context(tc.tile_pool(name="ring", bufs=4))
-        shared = ctx.enter_context(tc.tile_pool(name="shared", bufs=1))
-        psum = ctx.enter_context(tc.psum_pool(name="psum", bufs=4))
+        ring = ctx.enter_context(tc.tile_pool(name="ring", bufs=MEMBER_BUFS))
+        psum = ctx.enter_context(tc.psum_pool(name="psum", bufs=SLOTS))
 
         def held(shape, dtype, name, tag=None):
             return keep.tile(shape, dtype, name=name, tag=tag or name, align_bytes=64)
 
-        def weave(engine_copy, dst, src):
-            engine_copy(
-                dst.rearrange("p (c i) t -> p c t i", i=4),
-                src.rearrange("p t (c i) -> p c t i", i=4),
-            )
+        def scalar_cast(dst, src):
+            nc.scalar.activation(dst, src, ACT.Copy)
+
+        def weave(copy, woven, planes):
+            copy(woven.rearrange("p (c i) t -> p c t i", i=4), planes.rearrange("p t (c i) -> p c t i", i=4))
 
         def quantize(codes, scales, woven):
             nc.vector.quantize_mx(out=codes.bitcast(FP8X4), scales=scales, in_=woven.rearrange("p c t -> p (c t)"))
 
-        def product(acc, left_codes, left_scales, t, codes, scales):
+        def product(sums, left_codes, left_scales, panel, codes, scales):
             nc.tensor.matmul_mx(
-                out=acc,
-                lhsT=left_codes[:, t * P : (t + 1) * P].bitcast(FP8X4),
-                lhsT_scale=left_scales[:, t * P : (t + 1) * P],
-                rhs=codes[:].bitcast(FP8X4),
-                rhs_scale=scales[:],
+                out=sums,
+                lhsT=left_codes[:, panel * P : (panel + 1) * P].bitcast(FP8X4),
+                lhsT_scale=left_scales[:, panel * P : (panel + 1) * P],
+                rhs=codes.bitcast(FP8X4),
+                rhs_scale=scales,
                 start=True,
                 stop=True,
             )
 
-        offs_t = held([P, S // 16], U16, "offs_t")
-        n1_t = held([P, W // 16], U16, "n1_t")
-        n2_t = held([P, H // 16], U16, "n2_t")
-        n3_t = held([P, H // 16], U16, "n3_t")
-        xw_all = held([P, T], U32, "xw_all")
-        xs_all = held([P, T], U8, "xs_all")
-        wa_raw = [held([P, PACK, HALF], F32, f"wa_raw{a}") for a in range(2)]
-        w1_raw = held([P, PACK, H], F32, "w1_raw")
-        w2_raw = held([P, PACK, N], F32, "w2_raw")
-        res_t = held([P, PACK, H], F32, "res_t")
-        gt_t = held([P, PACK], F32, "gt_t")
-        gp_t = held([P, PACK], F32, "gp_t")
-        nc.gpsimd.memset(xs_all[:].bitcast(I32), 0)
+        def entries(list_tile, first, count):
+            return list_tile[:, first // PER_COLUMN : (first + count) // PER_COLUMN]
 
-        wa_rows = wa.rearrange("(p t) c -> p t c", t=PACK)
+        offs_t = held([P, S // PER_COLUMN], U16, "offs_t")
+        n1_t = held([P, W // PER_COLUMN], U16, "n1_t")
+        n2_t = held([P, H // PER_COLUMN], U16, "n2_t")
+        n3_t = held([P, H // PER_COLUMN], U16, "n3_t")
+        word_table = held([P, T], U32, "word_table")
+        scale_table = held([P, T], U8, "scale_table")
+        wa_raw = [held([P, SLOTS, HALF], F32, f"wa_raw{a}") for a in range(2)]
+        w1_raw = [held([P, SLOTS, HALF], F32, f"w1_raw{a}") for a in range(2)]
+        w2_raw = held([P, SLOTS, N], F32, "w2_raw")
+        res_t = held([P, N // P, H], F32, "res_t")
+        gt_t = held([P, SLOTS], F32, "gt_t")
+        gp_t = held([P, SLOTS], F32, "gp_t")
+
+        nc.gpsimd.memset(scale_table[:].bitcast(I32), 0)
+
+        wa_rows = wa.rearrange("(p t) c -> p t c", t=SLOTS)
+        w1_rows = w1.rearrange("(p t) c -> p t c", t=SLOTS)
         nc.sync.dma_start(offs_t[:], offs)
         nc.sync.dma_start(wa_raw[0][:], wa_rows[:, :, :HALF])
-        for q in range(4):
-            nc.sync.dma_start(
-                xs_all[q : P : 32, :].bitcast(I32), x_scales[0, q : 16 : 4, :].bitcast(I32)
-            )
-        nc.sync.dma_start(xw_all[:].bitcast(I32), x_words[0].rearrange("p n t -> p (n t)").bitcast(I32))
+        for r in range(4):
+            nc.sync.dma_start(scale_table[r:P:QUADRANT, :].bitcast(I32), x_scales[0, r : K // 32 : 4, :].bitcast(I32))
+        nc.sync.dma_start(word_table[:].bitcast(I32), x_words[0].rearrange("p n t -> p (n t)").bitcast(I32))
         nc.sync.dma_start(wa_raw[1][:], wa_rows[:, :, HALF:])
+        nc.sync.dma_start(w1_raw[0][:], w1_rows[:, :, :HALF])
         nc.sync.dma_start(n1_t[:], n1)
-        nc.sync.dma_start(w1_raw[:], w1.rearrange("(p t) c -> p t c", t=PACK))
-        nc.sync.dma_start(gt_t[:], gt.rearrange("(p t) o -> p (t o)", t=PACK))
-        nc.sync.dma_start(gp_t[:], gp.rearrange("(p t) o -> p (t o)", t=PACK))
+        nc.sync.dma_start(w1_raw[1][:], w1_rows[:, :, HALF:])
+        nc.sync.dma_start(gt_t[:], gt.rearrange("(p t) o -> p (t o)", t=SLOTS))
+        nc.sync.dma_start(gp_t[:], gp.rearrange("(p t) o -> p (t o)", t=SLOTS))
         nc.sync.dma_start(n3_t[:], n3)
         nc.sync.dma_start(n2_t[:], n2)
-        nc.sync.dma_start(w2_raw[:], w2.rearrange("(p t) c -> p t c", t=PACK))
+        nc.sync.dma_start(w2_raw[:], w2.rearrange("(p t) c -> p t c", t=SLOTS))
         nc.sync.dma_start(res_t[:], res.rearrange("(u p) c -> p u c", p=P))
 
         warm = held([P, 2], F32, "warm")
         nc.gpsimd.memset(warm[:, 0:1], 0.0)
         nc.scalar.activation(warm[:, 1:2], warm[:, 0:1], ACT.Sigmoid)
 
-        xs = held([P, S], U8, "xs")
-        nc.vector.tensor_copy(xs[:].rearrange("p (t m) -> p m t", t=PACK), xs_all[:].indirect(offs_t[:]))
+        x_scale = held([P, S], U8, "x_scale")
+        x_word = held([P, S], U32, "x_word")
+        nc.vector.tensor_copy(x_scale[:].rearrange("p (t m) -> p m t", t=SLOTS), scale_table[:].indirect(offs_t[:]))
+        nc.vector.tensor_copy(x_word[:].rearrange("p (t m) -> p m t", t=SLOTS), word_table[:].indirect(offs_t[:]))
 
-        y = [held([P, H], F32, f"y{t}", tag="wa_raw1" if t == 0 else None) for t in range(PACK)]
         wa_codes = held([P, H], U32, "wa_codes")
-        wa_scales = held([P, H], U8, "wa_scales", tag="xs_all")
-        for a in range(2):
-            woven = held([P, HALF, PACK], BF16, f"wa_woven{a}")
-            codes = wa_codes[:, a * HALF : (a + 1) * HALF]
-            scales = wa_scales[:, a * HALF : (a + 1) * HALF]
-            if a == 0:
-                nc.scalar.activation(
-                    woven[:].rearrange("p (c i) t -> p c t i", i=4),
-                    wa_raw[a][:].rearrange("p t (c i) -> p c t i", i=4),
-                    ACT.Copy,
-                )
-            else:
-                weave(nc.scalar.copy, woven[:, :SPLIT, :], wa_raw[a][:, :, :SPLIT])
-                weave(nc.vector.tensor_copy, woven[:, SPLIT:, :], wa_raw[a][:, :, SPLIT:])
-            quantize(codes, scales, woven[:])
-            if a == 0:
-                xw = held([P, S], U32, "xw", tag="wa_woven0")
-                nc.vector.tensor_copy(xw[:].rearrange("p (t m) -> p m t", t=PACK), xw_all[:].indirect(offs_t[:]))
-        for t in range(PACK):
-            copy = nc.scalar.copy if t in [0,3] else nc.vector.tensor_copy
-            bank = psum.tile([P, H], F32, name="y_bank", tag="wide")
-            step = HALF if t < 2 else H
-            for first in range(0, H, step):
-                cols = slice(first, first + step)
-                if t == 0 and first == 0:
-                    early = psum.tile([P, HALF], F32, name="y_early", tag="h_bank")
-                    product(early[:], xw, xs, t, wa_codes[:, cols], wa_scales[:, cols])
-                    copy(y[t][:, cols], early[:])
-                else:
-                    product(bank[:, cols], xw, xs, t, wa_codes[:, cols], wa_scales[:, cols])
-            rest = slice(HALF if t == 0 else 0, H)
-            copy(y[t][:, rest], bank[:, rest])
+        wa_scales = held([P, H], U8, "wa_scales", tag="scale_table")
+        halves = (slice(0, HALF), slice(HALF, H))
+        wa_woven = [held([P, HALF, SLOTS], BF16, f"wa_woven{a}") for a in range(2)]
+        weave(scalar_cast, wa_woven[0][:], wa_raw[0][:])
+        quantize(wa_codes[:, halves[0]], wa_scales[:, halves[0]], wa_woven[0][:])
+        weave(scalar_cast, wa_woven[1][:, :WA_ON_SCALAR, :], wa_raw[1][:, :, :WA_ON_SCALAR])
+        weave(nc.vector.tensor_copy, wa_woven[1][:, WA_ON_SCALAR:, :], wa_raw[1][:, :, WA_ON_SCALAR:])
+        quantize(wa_codes[:, halves[1]], wa_scales[:, halves[1]], wa_woven[1][:])
 
-        w1_woven = held([P, H, PACK], BF16, "w1_woven", tag="wa_codes")
+        def first_product(sums, t, cols):
+            product(sums, x_word, x_scale, t, wa_codes[:, cols], wa_scales[:, cols])
+
+        y = [held([P, H], F32, f"y{t}", tag="wa_raw1" if t == 0 else None) for t in range(SLOTS)]
+        y_bank = [psum.tile([P, H], F32, name=f"y_bank{t}", tag="wide") for t in range(SLOTS)]
+        y_early = psum.tile([P, HALF], F32, name="y_early", tag="h_bank")
+        first_product(y_early[:], 0, halves[0])
+        nc.scalar.copy(y[0][:, halves[0]], y_early[:])
+        first_product(y_bank[0][:, halves[1]], 0, halves[1])
+        nc.scalar.copy(y[0][:, halves[1]], y_bank[0][:, halves[1]])
+        for cols in halves:
+            first_product(y_bank[1][:, cols], 1, cols)
+        nc.vector.tensor_copy(y[1][:], y_bank[1][:])
+        first_product(y_bank[2][:], 2, slice(0, H))
+        nc.vector.tensor_copy(y[2][:], y_bank[2][:])
+        first_product(y_bank[3][:], 3, slice(0, H))
+        nc.vector.tensor_copy(y[3][:, halves[0]], y_bank[3][:, halves[0]])
+        nc.scalar.copy(y[3][:, halves[1]], y_bank[3][:, halves[1]])
+
+        w1_woven = held([P, H, SLOTS], BF16, "w1_woven")
         w1_codes = held([P, H], U32, "w1_codes")
         w1_scales = held([P, H], U8, "w1_scales")
-        w2_codes = held([P, N], U32, "w2_codes")
-        w2_scales = held([P, N], U8, "w2_scales")
-        last_larger = shared.tile([P, PACK, H], F32, name="last_larger", offset=0)
-        h_banks = []
-        nc.vector.tensor_copy(
-            w1_woven[:].rearrange("p (t m) j -> p m j t", t=PACK),
-            w1_raw[:].rearrange("p j (m t) -> p m j t", t=PACK),
-        )
+        dealt = w1_woven[:].rearrange("p (t m) j -> p m j t", t=SLOTS)
+        for a in range(2):
+            nc.vector.tensor_copy(
+                dealt[:, a * P // 2 : (a + 1) * P // 2], w1_raw[a][:].rearrange("p j (m t) -> p m j t", t=SLOTS)
+            )
         quantize(w1_codes[:], w1_scales[:], w1_woven[:])
 
-        b_start = [sum(B_CHUNKS[:c]) for c in range(len(B_CHUNKS))]
-        units = [(c, t) for c in range(len(B_CHUNKS)) for t in range(PACK)]
-        z_flat = [held([P, PACK, width], BF16, f"z_flat{c}") for c, width in enumerate(B_CHUNKS)]
-        gate, diff, smaller = {}, {}, {}
+        units = [(c, t) for c in range(CHUNKS) for t in range(SLOTS)]
+        z_planes = [held([P, SLOTS, CHUNK], BF16, f"z_planes{c}") for c in range(CHUNKS)]
+        smaller, gate, diff, z_woven = {}, {}, {}, {}
+        h_early = [psum.tile([P, LAST * CHUNK], F32, name="h_early", tag="h_bank") for t in range(SLOTS)]
+        h_last = []
 
         def extremes(c, t):
-            width = B_CHUNKS[c]
-            members = ring.tile([P, 2 * width], F32, name="members", align_bytes=64)
-            for e in range(0, 2 * width, 256):
-                n = min(256, 2 * width - e)
-                first = (2 * b_start[c] + e) // 16
-                nc.scalar.activation(
-                    members[:, e : e + n], y[t][:].indirect(n1_t[:, first : first + n // 16]), ACT.Copy
-                )
+            members = ring.tile([P, 2 * CHUNK], F32, name="members", align_bytes=64)
+            nc.scalar.activation(members[:], y[t][:].indirect(entries(n1_t, 2 * c * CHUNK, 2 * CHUNK)), ACT.Copy)
             pairs = members[:].rearrange("p (j e) -> p j e", e=2)
-            if c + 1 < len(B_CHUNKS):
-                larger = held([P, width], F32, f"larger{c}_{t}")[:]
-            else:
-                larger = last_larger[:, t, :width]
-            smaller[c, t] = held([P, width], F32, f"smaller{c}_{t}")
-            gate[c, t] = held([P, width], F32, f"gate{c}_{t}")
-            nc.vector.tensor_tensor(larger, pairs[:, :, 0], pairs[:, :, 1], ALU.max)
+            larger = held([P, CHUNK], F32, f"larger{c}_{t}")
+            smaller[c, t] = held([P, CHUNK], F32, f"smaller{c}_{t}")
+            gate[c, t] = held([P, CHUNK], F32, f"gate{c}_{t}")
+            nc.vector.tensor_tensor(larger[:], pairs[:, :, 0], pairs[:, :, 1], ALU.max)
             nc.vector.tensor_tensor(smaller[c, t][:], pairs[:, :, 0], pairs[:, :, 1], ALU.min)
-            nc.scalar.activation(gate[c, t][:], larger, ACT.Sigmoid)
+            nc.scalar.activation(gate[c, t][:], larger[:], ACT.Sigmoid)
 
         def difference(c, t):
-            width = B_CHUNKS[c]
-            diff[c, t] = held([P, width], F32, f"diff{c}_{t}")
+            diff[c, t] = held([P, CHUNK], F32, f"diff{c}_{t}")
             nc.vector.tensor_tensor(
-                diff[c, t][:], y[t][:, b_start[c] : b_start[c] + width], smaller[c, t][:], ALU.subtract
+                diff[c, t][:], y[t][:, c * CHUNK : (c + 1) * CHUNK], smaller[c, t][:], ALU.subtract
             )
 
         def make_z(c, t):
             nc.vector.scalar_tensor_tensor(
-                z_flat[c][:, t, :], diff[c, t][:], gt_t[:, t : t + 1], gate[c, t][:], ALU.mult, ALU.mult
+                z_planes[c][:, t, :], diff[c, t][:], gt_t[:, t : t + 1], gate[c, t][:], ALU.mult, ALU.mult
             )
 
+        def weave_z(c):
+            z_woven[c] = held([P, CHUNK, SLOTS], BF16, f"z_woven{c}")
+            weave(nc.vector.tensor_copy, z_woven[c][:], z_planes[c][:])
+
         def second_product(c):
-            width = B_CHUNKS[c]
-            last = c + 1 == len(B_CHUNKS)
-            woven = held([P, width, PACK], BF16, f"z_woven{c}", tag="late" if last else None)
-            weave(nc.vector.tensor_copy, woven[:], z_flat[c][:])
-            codes = held([P, width], U32, f"z_codes{c}")
-            scales = held([P, width], U8, f"z_scales{c}")
-            return woven, codes, scales
+            codes = held([P, CHUNK], U32, f"z_codes{c}")
+            scales = held([P, CHUNK], U8, f"z_scales{c}")
+            quantize(codes[:], scales[:], z_woven[c][:])
+            for t in range(SLOTS):
+                if c < LAST:
+                    sums = h_early[t][:, c * CHUNK : (c + 1) * CHUNK]
+                else:
+                    h_last.append(psum.tile([P, CHUNK], F32, name="h_last", tag="wide"))
+                    sums = h_last[t][:]
+                product(sums, w1_codes, w1_scales, t, codes[:], scales[:])
 
-        def second_matmuls(c, woven, codes, scales):
-            width = B_CHUNKS[c]
-            quantize(codes[:], scales[:], woven[:])
-            last = c + 1 == len(B_CHUNKS)
-            per_bank = 1 if last else H // width
-            for t0 in range(0, PACK, per_bank):
-                ts = range(t0, min(PACK, t0 + per_bank))
-                bank = psum.tile([P, len(ts), width], F32, name="h_bank", tag="wide" if last else "h_bank")
-                for t in ts:
-                    product(bank[:, t - t0, :], w1_codes, w1_scales, t, codes, scales)
-                h_banks.extend((c, t, bank[:, t - t0, :]) for t in ts)
+        def unit(u):
+            return units[u] if 0 <= u < len(units) else None
 
-        staged = {}
+        def closed_chunk(u):
+            return units[u][0] if unit(u) and units[u][1] == SLOTS - 1 else None
+
         for u in range(len(units) + LAG + 2):
-            if u < len(units):
-                extremes(*units[u])
-            if 0 <= u - LAG - 2 < len(units) and units[u - LAG - 2][1] == PACK - 1:
-                c = units[u - LAG - 2][0]
-                second_matmuls(c, *staged[c])
-            if 0 <= u - LAG - 1 < len(units) and units[u - LAG - 1][1] == PACK - 1:
-                c = units[u - LAG - 1][0]
-                staged[c] = second_product(c)
-            if 0 <= u - LAG < len(units):
-                make_z(*units[u - LAG])
-            if 0 <= u - 1 < len(units):
-                difference(*units[u - 1])
+            if unit(u):
+                extremes(*unit(u))
+            if closed_chunk(u - LAG - 2) is not None:
+                second_product(closed_chunk(u - LAG - 2))
+            if closed_chunk(u - LAG - 1) is not None:
+                weave_z(closed_chunk(u - LAG - 1))
+            if unit(u - LAG):
+                make_z(*unit(u - LAG))
+            if unit(u - 1):
+                difference(*unit(u - 1))
 
-        for a, (copy, tag) in enumerate(((nc.scalar.copy, "gate3_0"), (nc.vector.tensor_copy, "late"))):
-            cols = slice(a * HALF, (a + 1) * HALF)
-            w2_woven = held([P, HALF, PACK], BF16, f"w2_woven{a}", tag=tag)
-            weave(copy, w2_woven[:], w2_raw[:, :, cols])
-            quantize(w2_codes[:, cols], w2_scales[:, cols], w2_woven[:])
-        h = [shared.tile([P, H], F32, name=f"h{t}", offset=t * H * 4) for t in range(PACK)]
-        for c, t, sums in h_banks:
-            place = h[t][:, b_start[c] : b_start[c] + B_CHUNKS[c]]
-            if False:
-                nc.vector.tensor_scalar(place, sums, gp_t[:, t : t + 1], None, ALU.mult)
-            else:
-                nc.scalar.activation(place, sums, ACT.Copy, scale=gp_t[:, t : t + 1])
+        w2_codes = held([P, N], U32, "w2_codes")
+        w2_scales = held([P, N], U8, "w2_scales")
+        for a, (copy, tag) in enumerate(
+            ((scalar_cast, f"gate{LAST - 1}_{SLOTS - 1}"), (nc.vector.tensor_copy, f"z_woven{LAST}"))
+        ):
+            w2_woven = held([P, HALF, SLOTS], BF16, f"w2_woven{a}", tag=tag)
+            weave(copy, w2_woven[:], w2_raw[:, :, halves[a]])
+            quantize(w2_codes[:, halves[a]], w2_scales[:, halves[a]], w2_woven[:])
+
+        h = [held([P, H], F32, f"h{t}") for t in range(SLOTS)]
+        for t in range(SLOTS):
+            nc.scalar.activation(h[t][:, : LAST * CHUNK], h_early[t][:], ACT.Copy, scale=gp_t[:, t : t + 1])
+        for t in range(SLOTS):
+            nc.scalar.activation(h[t][:, LAST * CHUNK :], h_last[t][:], ACT.Copy, scale=gp_t[:, t : t + 1])
 
         out_rows = out.rearrange("(u p) c -> p u c", p=P)
-        c_start = [sum(C_CHUNKS[:c]) for c in range(len(C_CHUNKS))]
-        third, second, z2_woven, o_bank = {}, {}, {}, {}
+        panels = N // P
+        at_n3, at_n2, z2_woven, out_banks = {}, {}, {}, {}
 
         def fetch_n3(c):
-            width = C_CHUNKS[c]
-            first = c_start[c] // 16
-            third[c] = held([P, PACK, width], F32, f"third{c}")
-            for t in range(PACK):
+            at_n3[c] = held([P, SLOTS, CHUNK], F32, f"at_n3_{c}")
+            for t in range(SLOTS):
                 nc.scalar.activation(
-                    third[c][:, t, :], h[t][:].indirect(n3_t[:, first : first + width // 16]), ACT.Copy, scale=0.75
+                    at_n3[c][:, t, :], h[t][:].indirect(entries(n3_t, c * CHUNK, CHUNK)), ACT.Copy, scale=0.75
                 )
 
         def fetch_n2(c):
-            width = C_CHUNKS[c]
-            first = c_start[c] // 16
-            second[c] = ring.tile([P, PACK, width], F32, name="second", align_bytes=64, bufs=2)
-            for t in range(PACK):
-                window = h[t][:].indirect(n2_t[:, first : first + width // 16])
-                if c + 1 < len(C_CHUNKS):
-                    nc.vector.tensor_copy(second[c][:, t, :], window)
+            at_n2[c] = ring.tile([P, SLOTS, CHUNK], F32, name="at_n2", align_bytes=64, bufs=SECOND_BUFS)
+            for t in range(SLOTS):
+                window = h[t][:].indirect(entries(n2_t, c * CHUNK, CHUNK))
+                if c < LAST:
+                    nc.vector.tensor_copy(at_n2[c][:, t, :], window)
                 else:
-                    nc.scalar.activation(second[c][:, t, :], window, ACT.Copy)
+                    nc.scalar.activation(at_n2[c][:, t, :], window, ACT.Copy)
 
-        def weave_z2(c):
-            z2_woven[c] = held([P, C_CHUNKS[c], PACK], BF16, f"z2_woven{c}")
+        def make_z2(c):
+            z2_woven[c] = held([P, CHUNK, SLOTS], BF16, f"z2_woven{c}")
             nc.vector.tensor_tensor(
                 z2_woven[c][:].rearrange("p (c i) t -> p c t i", i=2),
-                second[c][:].rearrange("p t (c i) -> p c t i", i=2),
-                third[c][:].rearrange("p t (c i) -> p c t i", i=2),
+                at_n2[c][:].rearrange("p t (c i) -> p c t i", i=2),
+                at_n3[c][:].rearrange("p t (c i) -> p c t i", i=2),
                 ALU.add,
             )
 
         def third_product(c):
-            width = C_CHUNKS[c]
-            codes = held([P, width], U32, f"z2_codes{c}")
-            scales = held([P, width], U8, f"z2_scales{c}")
+            codes = held([P, CHUNK], U32, f"z2_codes{c}")
+            scales = held([P, CHUNK], U8, f"z2_scales{c}")
             quantize(codes[:], scales[:], z2_woven[c][:])
-            per_bank = H // width if c + 2 < len(C_CHUNKS) else 2
-            o_bank[c] = []
-            for u0 in range(0, PACK, per_bank):
-                us = range(u0, min(PACK, u0 + per_bank))
-                bank = psum.tile([P, len(us), width], F32, name="o_bank", tag="wide")
-                o_bank[c].append((us, bank))
-                for u in us:
-                    product(bank[:, u - u0, :], w2_codes, w2_scales, u, codes, scales)
+            per_bank = panels if c < LAST - 1 else panels // 2
+            out_banks[c] = []
+            for first in range(0, panels, per_bank):
+                bank = psum.tile([P, per_bank, CHUNK], F32, name="out_bank", tag="wide")
+                out_banks[c].append((slice(first, first + per_bank), bank))
+                for i in range(per_bank):
+                    product(bank[:, i, :], w2_codes, w2_scales, first + i, codes[:], scales[:])
 
         def finish(c):
-            cols = slice(c_start[c], c_start[c] + C_CHUNKS[c])
-            for us, bank in o_bank[c]:
-                result = held([P, len(us), C_CHUNKS[c]], F32, f"result{c}_{us.start}")
-                nc.vector.tensor_tensor(result[:], bank[:], res_t[:, us.start : us.stop, cols], ALU.add)
-                nc.sync.dma_start(out_rows[:, us.start : us.stop, cols], result[:])
+            cols = slice(c * CHUNK, (c + 1) * CHUNK)
+            for us, bank in out_banks[c]:
+                result = held([P, us.stop - us.start, CHUNK], F32, f"result{c}_{us.start}")
+                nc.vector.tensor_tensor(result[:], bank[:], res_t[:, us, cols], ALU.add)
+                nc.sync.dma_start(out_rows[:, us, cols], result[:])
 
-        last = len(C_CHUNKS) - 1
-        for c in range(len(C_CHUNKS) + 2):
-            if c <= last:
+        for c in range(CHUNKS + 2):
+            if c <= LAST:
                 fetch_n3(c)
                 fetch_n2(c)
-            if 1 <= c <= last + 1:
+            if 1 <= c <= CHUNKS:
                 third_product(c - 1)
-            if c <= last:
-                weave_z2(c)
+            if c <= LAST:
+                make_z2(c)
             if c >= 2:
                 finish(c - 2)

from contextlib import ExitStack

import concourse.mybir as mybir

K, T, S, N, H, W = 512, 2048, 512, 512, 512, 1024
FLOPS = 2 * K * S * H + 2 * S * H * H + 2 * H * N * H

F32 = mybir.dt.float32
BF16 = mybir.dt.bfloat16
I32 = mybir.dt.int32
U32 = mybir.dt.uint32
U16 = mybir.dt.uint16
U8 = mybir.dt.uint8
FP8X4 = mybir.dt.float8_e4m3fn_x4
ALU = mybir.AluOpType
ACT = mybir.ActivationFunctionType

P = 128
SLOTS = 4
QUADRANT = 32
PER_COLUMN = 16
HALF = H // 2
CHUNK = 128
CHUNKS = H // CHUNK
LAST = CHUNKS - 1
WA_ON_SCALAR = 112
MEMBER_BUFS = 4
LAG = 3
SECOND_BUFS = 2


def tile_picked_tok2ghardsum_none_p_kernel(
    tc, x_words, x_scales, wa, gt, w1, gp, res, w2, offs, n1, n2, n3, out
):
    nc = tc.nc
    with ExitStack() as ctx:
        keep = ctx.enter_context(tc.tile_pool(name="keep", bufs=1))
        ring = ctx.enter_context(tc.tile_pool(name="ring", bufs=MEMBER_BUFS))
        psum = ctx.enter_context(tc.psum_pool(name="psum", bufs=SLOTS))

        def held(shape, dtype, name, tag=None):
            return keep.tile(shape, dtype, name=name, tag=tag or name, align_bytes=64)

        def scalar_cast(dst, src):
            nc.scalar.activation(dst, src, ACT.Copy)

        def weave(copy, woven, planes):
            copy(woven.rearrange("p (c i) t -> p c t i", i=4), planes.rearrange("p t (c i) -> p c t i", i=4))

        def quantize(codes, scales, woven):
            nc.vector.quantize_mx(out=codes.bitcast(FP8X4), scales=scales, in_=woven.rearrange("p c t -> p (c t)"))

        def product(sums, left_codes, left_scales, panel, codes, scales):
            nc.tensor.matmul_mx(
                out=sums,
                lhsT=left_codes[:, panel * P : (panel + 1) * P].bitcast(FP8X4),
                lhsT_scale=left_scales[:, panel * P : (panel + 1) * P],
                rhs=codes.bitcast(FP8X4),
                rhs_scale=scales,
                start=True,
                stop=True,
            )

        def entries(list_tile, first, count):
            return list_tile[:, first // PER_COLUMN : (first + count) // PER_COLUMN]

        offs_t = held([P, S // PER_COLUMN], U16, "offs_t")
        n1_t = held([P, W // PER_COLUMN], U16, "n1_t")
        n2_t = held([P, H // PER_COLUMN], U16, "n2_t")
        n3_t = held([P, H // PER_COLUMN], U16, "n3_t")
        word_table = held([P, T], U32, "word_table")
        scale_table = held([P, T], U8, "scale_table")
        wa_raw = [held([P, SLOTS, HALF], F32, f"wa_raw{a}") for a in range(2)]
        w1_raw = [held([P, SLOTS, HALF], F32, f"w1_raw{a}") for a in range(2)]
        w2_raw = held([P, SLOTS, N], F32, "w2_raw")
        res_t = held([P, N // P, H], F32, "res_t")
        gt_t = held([P, SLOTS], F32, "gt_t")
        gp_t = held([P, SLOTS], F32, "gp_t")

        nc.gpsimd.memset(scale_table[:].bitcast(I32), 0)

        wa_rows = wa.rearrange("(p t) c -> p t c", t=SLOTS)
        w1_rows = w1.rearrange("(p t) c -> p t c", t=SLOTS)
        nc.sync.dma_start(offs_t[:], offs)
        nc.sync.dma_start(wa_raw[0][:], wa_rows[:, :, :HALF])
        for r in range(4):
            nc.sync.dma_start(scale_table[r:P:QUADRANT, :].bitcast(I32), x_scales[0, r : K // 32 : 4, :].bitcast(I32))
        nc.sync.dma_start(word_table[:].bitcast(I32), x_words[0].rearrange("p n t -> p (n t)").bitcast(I32))
        nc.sync.dma_start(wa_raw[1][:], wa_rows[:, :, HALF:])
        nc.sync.dma_start(w1_raw[0][:], w1_rows[:, :, :HALF])
        nc.sync.dma_start(n1_t[:], n1)
        nc.sync.dma_start(w1_raw[1][:], w1_rows[:, :, HALF:])
        nc.sync.dma_start(gt_t[:], gt.rearrange("(p t) o -> p (t o)", t=SLOTS))
        nc.sync.dma_start(gp_t[:], gp.rearrange("(p t) o -> p (t o)", t=SLOTS))
        nc.sync.dma_start(n3_t[:], n3)
        nc.sync.dma_start(n2_t[:], n2)
        nc.sync.dma_start(w2_raw[:], w2.rearrange("(p t) c -> p t c", t=SLOTS))
        nc.sync.dma_start(res_t[:], res.rearrange("(u p) c -> p u c", p=P))

        warm = held([P, 2], F32, "warm")
        nc.gpsimd.memset(warm[:, 0:1], 0.0)
        nc.scalar.activation(warm[:, 1:2], warm[:, 0:1], ACT.Sigmoid)

        x_scale = held([P, S], U8, "x_scale")
        x_word = held([P, S], U32, "x_word")
        nc.vector.tensor_copy(x_scale[:].rearrange("p (t m) -> p m t", t=SLOTS), scale_table[:].indirect(offs_t[:]))
        nc.vector.tensor_copy(x_word[:].rearrange("p (t m) -> p m t", t=SLOTS), word_table[:].indirect(offs_t[:]))

        wa_codes = held([P, H], U32, "wa_codes")
        wa_scales = held([P, H], U8, "wa_scales", tag="scale_table")
        halves = (slice(0, HALF), slice(HALF, H))
        wa_woven = [held([P, HALF, SLOTS], BF16, f"wa_woven{a}") for a in range(2)]
        weave(scalar_cast, wa_woven[0][:], wa_raw[0][:])
        quantize(wa_codes[:, halves[0]], wa_scales[:, halves[0]], wa_woven[0][:])
        weave(scalar_cast, wa_woven[1][:, :WA_ON_SCALAR, :], wa_raw[1][:, :, :WA_ON_SCALAR])
        weave(nc.vector.tensor_copy, wa_woven[1][:, WA_ON_SCALAR:, :], wa_raw[1][:, :, WA_ON_SCALAR:])
        quantize(wa_codes[:, halves[1]], wa_scales[:, halves[1]], wa_woven[1][:])

        def first_product(sums, t, cols):
            product(sums, x_word, x_scale, t, wa_codes[:, cols], wa_scales[:, cols])

        y = [held([P, H], F32, f"y{t}", tag="wa_raw1" if t == 0 else None) for t in range(SLOTS)]
        y_bank = [psum.tile([P, H], F32, name=f"y_bank{t}", tag="wide") for t in range(SLOTS)]
        y_early = psum.tile([P, HALF], F32, name="y_early", tag="h_bank")
        first_product(y_early[:], 0, halves[0])
        nc.scalar.copy(y[0][:, halves[0]], y_early[:])
        first_product(y_bank[0][:, halves[1]], 0, halves[1])
        nc.scalar.copy(y[0][:, halves[1]], y_bank[0][:, halves[1]])
        for cols in halves:
            first_product(y_bank[1][:, cols], 1, cols)
        nc.vector.tensor_copy(y[1][:], y_bank[1][:])
        first_product(y_bank[2][:], 2, slice(0, H))
        nc.vector.tensor_copy(y[2][:], y_bank[2][:])
        first_product(y_bank[3][:], 3, slice(0, H))
        nc.vector.tensor_copy(y[3][:, halves[0]], y_bank[3][:, halves[0]])
        nc.scalar.copy(y[3][:, halves[1]], y_bank[3][:, halves[1]])

        w1_woven = held([P, H, SLOTS], BF16, "w1_woven")
        w1_codes = held([P, H], U32, "w1_codes")
        w1_scales = held([P, H], U8, "w1_scales")
        dealt = w1_woven[:].rearrange("p (t m) j -> p m j t", t=SLOTS)
        for a in range(2):
            nc.vector.tensor_copy(
                dealt[:, a * P // 2 : (a + 1) * P // 2], w1_raw[a][:].rearrange("p j (m t) -> p m j t", t=SLOTS)
            )
        quantize(w1_codes[:], w1_scales[:], w1_woven[:])

        units = [(c, t) for c in range(CHUNKS) for t in range(SLOTS)]
        z_planes = [held([P, SLOTS, CHUNK], BF16, f"z_planes{c}") for c in range(CHUNKS)]
        smaller, gate, diff, z_woven = {}, {}, {}, {}
        h_early = [psum.tile([P, LAST * CHUNK], F32, name="h_early", tag="h_bank") for t in range(SLOTS)]
        h_last = []

        def extremes(c, t):
            members = ring.tile([P, 2 * CHUNK], F32, name="members", align_bytes=64)
            nc.scalar.activation(members[:], y[t][:].indirect(entries(n1_t, 2 * c * CHUNK, 2 * CHUNK)), ACT.Copy)
            pairs = members[:].rearrange("p (j e) -> p j e", e=2)
            larger = held([P, CHUNK], F32, f"larger{c}_{t}")
            smaller[c, t] = held([P, CHUNK], F32, f"smaller{c}_{t}")
            gate[c, t] = held([P, CHUNK], F32, f"gate{c}_{t}")
            nc.vector.tensor_tensor(larger[:], pairs[:, :, 0], pairs[:, :, 1], ALU.max)
            nc.vector.tensor_tensor(smaller[c, t][:], pairs[:, :, 0], pairs[:, :, 1], ALU.min)
            nc.scalar.activation(gate[c, t][:], larger[:], ACT.Sigmoid)

        def difference(c, t):
            diff[c, t] = held([P, CHUNK], F32, f"diff{c}_{t}")
            nc.vector.tensor_tensor(
                diff[c, t][:], y[t][:, c * CHUNK : (c + 1) * CHUNK], smaller[c, t][:], ALU.subtract
            )

        def make_z(c, t):
            nc.vector.scalar_tensor_tensor(
                z_planes[c][:, t, :], diff[c, t][:], gt_t[:, t : t + 1], gate[c, t][:], ALU.mult, ALU.mult
            )

        def weave_z(c):
            z_woven[c] = held([P, CHUNK, SLOTS], BF16, f"z_woven{c}")
            weave(nc.vector.tensor_copy, z_woven[c][:], z_planes[c][:])

        def second_product(c):
            codes = held([P, CHUNK], U32, f"z_codes{c}")
            scales = held([P, CHUNK], U8, f"z_scales{c}")
            quantize(codes[:], scales[:], z_woven[c][:])
            for t in range(SLOTS):
                if c < LAST:
                    sums = h_early[t][:, c * CHUNK : (c + 1) * CHUNK]
                else:
                    h_last.append(psum.tile([P, CHUNK], F32, name="h_last", tag="wide"))
                    sums = h_last[t][:]
                product(sums, w1_codes, w1_scales, t, codes[:], scales[:])

        def unit(u):
            return units[u] if 0 <= u < len(units) else None

        def closed_chunk(u):
            return units[u][0] if unit(u) and units[u][1] == SLOTS - 1 else None

        for u in range(len(units) + LAG + 2):
            if unit(u):
                extremes(*unit(u))
            if closed_chunk(u - LAG - 2) is not None:
                second_product(closed_chunk(u - LAG - 2))
            if closed_chunk(u - LAG - 1) is not None:
                weave_z(closed_chunk(u - LAG - 1))
            if unit(u - LAG):
                make_z(*unit(u - LAG))
            if unit(u - 1):
                difference(*unit(u - 1))

        w2_codes = held([P, N], U32, "w2_codes")
        w2_scales = held([P, N], U8, "w2_scales")
        for a, (copy, tag) in enumerate(
            ((scalar_cast, f"gate{LAST - 1}_{SLOTS - 1}"), (nc.vector.tensor_copy, f"z_woven{LAST}"))
        ):
            w2_woven = held([P, HALF, SLOTS], BF16, f"w2_woven{a}", tag=tag)
            weave(copy, w2_woven[:], w2_raw[:, :, halves[a]])
            quantize(w2_codes[:, halves[a]], w2_scales[:, halves[a]], w2_woven[:])

        h = [held([P, H], F32, f"h{t}") for t in range(SLOTS)]
        for t in range(SLOTS):
            nc.scalar.activation(h[t][:, : LAST * CHUNK], h_early[t][:], ACT.Copy, scale=gp_t[:, t : t + 1])
        for t in range(SLOTS):
            nc.scalar.activation(h[t][:, LAST * CHUNK :], h_last[t][:], ACT.Copy, scale=gp_t[:, t : t + 1])

        out_rows = out.rearrange("(u p) c -> p u c", p=P)
        panels = N // P
        at_n3, at_n2, z2_woven, out_banks = {}, {}, {}, {}

        def fetch_n3(c):
            at_n3[c] = held([P, SLOTS, CHUNK], F32, f"at_n3_{c}")
            for t in range(SLOTS):
                nc.scalar.activation(
                    at_n3[c][:, t, :], h[t][:].indirect(entries(n3_t, c * CHUNK, CHUNK)), ACT.Copy, scale=0.75
                )

        def fetch_n2(c):
            at_n2[c] = ring.tile([P, SLOTS, CHUNK], F32, name="at_n2", align_bytes=64, bufs=SECOND_BUFS)
            for t in range(SLOTS):
                window = h[t][:].indirect(entries(n2_t, c * CHUNK, CHUNK))
                if c < LAST:
                    nc.vector.tensor_copy(at_n2[c][:, t, :], window)
                else:
                    nc.scalar.activation(at_n2[c][:, t, :], window, ACT.Copy)

        def make_z2(c):
            z2_woven[c] = held([P, CHUNK, SLOTS], BF16, f"z2_woven{c}")
            nc.vector.tensor_tensor(
                z2_woven[c][:].rearrange("p (c i) t -> p c t i", i=2),
                at_n2[c][:].rearrange("p t (c i) -> p c t i", i=2),
                at_n3[c][:].rearrange("p t (c i) -> p c t i", i=2),
                ALU.add,
            )

        def third_product(c):
            codes = held([P, CHUNK], U32, f"z2_codes{c}")
            scales = held([P, CHUNK], U8, f"z2_scales{c}")
            quantize(codes[:], scales[:], z2_woven[c][:])
            per_bank = panels if c < LAST - 1 else panels // 2
            out_banks[c] = []
            for first in range(0, panels, per_bank):
                bank = psum.tile([P, per_bank, CHUNK], F32, name="out_bank", tag="wide")
                out_banks[c].append((slice(first, first + per_bank), bank))
                for i in range(per_bank):
                    product(bank[:, i, :], w2_codes, w2_scales, first + i, codes[:], scales[:])

        def finish(c):
            cols = slice(c * CHUNK, (c + 1) * CHUNK)
            for us, bank in out_banks[c]:
                result = held([P, us.stop - us.start, CHUNK], F32, f"result{c}_{us.start}")
                nc.vector.tensor_tensor(result[:], bank[:], res_t[:, us, cols], ALU.add)
                nc.sync.dma_start(out_rows[:, us, cols], result[:])

        for c in range(CHUNKS + 2):
            if c <= LAST:
                fetch_n3(c)
                fetch_n2(c)
            if 1 <= c <= CHUNKS:
                third_product(c - 1)
            if c <= LAST:
                make_z2(c)
            if c >= 2:
                finish(c - 2)
